import numpy as np
import ml_dtypes


def mxq(x, axis, fmt="e4m3"):
    dtype, down = {"e4m3": (ml_dtypes.float8_e4m3fn, 7), "e5m2": (ml_dtypes.float8_e5m2, 14)}[fmt]
    v = np.moveaxis(np.asarray(x, np.float32).astype(ml_dtypes.bfloat16).astype(np.float64), axis, -1)
    blocks = v.reshape(v.shape[:-1] + (-1, 32))
    amax = np.abs(blocks).max(-1, keepdims=True)
    byte = np.maximum(np.where(amax > 0, np.frexp(amax)[1] - 1 + 127, 0) - down, 1)
    scale = np.exp2(byte - 127.0)
    codes = (blocks / scale).astype(np.float32).astype(dtype).astype(np.float64)
    return np.moveaxis((codes * scale).reshape(v.shape), -1, axis)


WIDE = False


def mx_kscale(k):
    if not WIDE:
        return np.ones(k)
    levels = np.array([10, -10, 5, -5, 0])
    if k % 512:
        return np.exp2(np.random.permutation(np.resize(levels, k // 32))).repeat(32)
    a = np.empty((k // 512, 16))
    for p in range(k // 512):
        a[p, :8] = np.random.permutation(np.resize(levels, 8))
        for g in range(8):
            far = levels[np.abs(levels - a[p, g]) >= 10]
            a[p, g + 8] = far[np.random.randint(len(far))]
    return np.exp2(a.ravel()).repeat(32)


def f64(x):
    return np.asarray(x).astype(np.float64)


def striped(idx):
    return np.tile(idx.reshape(-1, 16).T, (8, 1)).astype(np.uint16)


def unstriped(offs):
    return offs[:16].T.reshape(-1).astype(np.int64)


def relu(v):
    return np.maximum(v, 0.0)


K, T, E, C, H, N = 1024, 1024, 2, 256, 512, 128


def by_expert(wq, xq):
    return np.concatenate([wq[e].T @ xq[:, e * C:(e + 1) * C] for e in range(E)], axis=1)


def setup_inputs():
    n = np.random.standard_normal
    s = mx_kscale(K)[:, None]
    u = mx_kscale(H)
    return {
        "xT": (n((K, T)) * s).astype(np.float32),
        "xr": n((N, T)).astype(np.float32),
        "w1": (n((E, K, H)) / np.sqrt(K) / s[None]).astype(np.float32),
        "w3": (n((E, K, H)) / np.sqrt(K) / s[None] * u[None, None, :]).astype(np.float32),
        "w2": (n((E, H, N)) / np.sqrt(H) / u[None, :, None]).astype(np.float32),
        "gate": np.tile(np.random.uniform(0.2, 1.0, E * C), (N, 1)).astype(np.float32),
        "offs": striped(np.random.permutation(T)[:E * C]),
    }


def reference(xT, xr, w1, w3, w2, gate, offs):
    idx = unstriped(offs)
    xq = mxq(f64(xT)[:, idx], 0, "e4m3")
    h = relu(by_expert(mxq(f64(w1), 1, "e4m3"), xq))
    h = h * by_expert(mxq(f64(w3), 1, "e4m3"), xq)
    y = by_expert(mxq(f64(w2), 1, "e4m3"), mxq(h, 0, "e4m3"))
    out = f64(xr).copy()
    out[:, idx] += f64(gate) * y
    return out

@@ -1,0 +1,256 @@
+from contextlib import ExitStack
+
+import concourse.mybir as mybir
+
+K, T, E, C, H, N = 1024, 1024, 2, 256, 512, 128
+S = E * C
+FLOPS = 2 * S * (2 * K * H + H * N)
+
+P = 128
+PACK = 4
+K_PASS = P * PACK
+PASSES = K // K_PASS
+BLK = 128
+HALF = T // 2
+
+F32 = mybir.dt.float32
+BF16 = mybir.dt.bfloat16
+U32 = mybir.dt.uint32
+U16 = mybir.dt.uint16
+U8 = mybir.dt.uint8
+FP8X4 = mybir.dt.float8_e4m3fn_x4
+COPY = mybir.ActivationFunctionType.Copy
+RELU = mybir.ActivationFunctionType.Relu
+MULT = mybir.AluOpType.mult
+ADD = mybir.AluOpType.add
+
+
+def tile_moe_res_glu_relu_kernel(tc, xT, xr, w1, w3, w2, gate, offs, out):
+    nc = tc.nc
+    with ExitStack() as ctx:
+        keep = ctx.enter_context(tc.tile_pool(name="keep", bufs=1))
+        psum = ctx.enter_context(tc.psum_pool(name="psum", bufs=6))
+        psum_y = ctx.enter_context(tc.psum_pool(name="psum_y", bufs=2))
+
+        offsets = keep.tile([P, S // 16], U16, name="offsets")
+        nc.sync.dma_start(offsets[:], offs)
+
+        x_raw = {}
+        x_bf = {}
+        for s in range(PASSES):
+            for h in range(2):
+                x_raw[s, h] = keep.tile([P, PACK, HALF], F32, name=f"x_raw{s}{h}")
+                x_bf[s, h] = keep.tile([P, HALF, PACK], BF16, name=f"x_bf{s}{h}", align_bytes=64)
+        x_words = [keep.tile([P, T], U32, name=f"x_words{s}", align_bytes=64) for s in range(PASSES)]
+        x_bytes = keep.tile([P, T], U8, name="x_bytes", align_bytes=64)
+        slot_words = [keep.tile([P, S], U32, name=f"slot_words{s}", align_bytes=64) for s in range(PASSES)]
+        slot_bytes = keep.tile([P, S], U8, name="slot_bytes", align_bytes=64)
+        window = keep.tile([P, T], F32, name="window")
+        nc.gpsimd.memset(x_bytes[:], 0)
+        nc.gpsimd.memset(window[:], 0.0)
+
+        w_raw, w_bf, w_codes, w_scales = {}, {}, {}, {}
+        for e in range(E):
+            for g in range(2):
+                for s in range(PASSES):
+                    key = (e, g, s)
+                    w_raw[key] = keep.tile([P, PACK, H], F32, name=f"w_raw{e}{g}{s}")
+                    w_bf[key] = keep.tile([P, H * PACK], BF16, name=f"w_bf{e}{g}{s}", align_bytes=64)
+                    w_codes[key] = keep.tile([P, H], U32, name=f"w_codes{e}{g}{s}", align_bytes=64)
+                    w_scales[key] = keep.tile([P, H], U8, name=f"w_scales{e}{g}{s}", align_bytes=64)
+        w2_raw = [keep.tile([P, PACK, N], F32, name=f"w2_raw{e}") for e in range(E)]
+        w2_bf = [keep.tile([P, N, PACK], BF16, name=f"w2_bf{e}", align_bytes=64) for e in range(E)]
+        w2_codes = [keep.tile([P, N], U32, name=f"w2_codes{e}", align_bytes=64) for e in range(E)]
+        w2_scales = [keep.tile([P, N], U8, name=f"w2_scales{e}", align_bytes=64) for e in range(E)]
+        gate_sb = [keep.tile([P, C], F32, name=f"gate{e}") for e in range(E)]
+        xr_sb = keep.tile([P, T], F32, name="xr_sb")
+
+        weights = (w1, w3)
+
+        def load_x(s, h):
+            rows = xT[s * K_PASS : (s + 1) * K_PASS, h * HALF : (h + 1) * HALF]
+            nc.sync.dma_start(x_raw[s, h][:], rows.rearrange("(p j) w -> p j w", j=PACK))
+
+        def load_w(e, g, s, lo, hi):
+            rows = weights[g][e][s * K_PASS : (s + 1) * K_PASS, lo:hi]
+            nc.sync.dma_start(w_raw[e, g, s][:, :, lo:hi], rows.rearrange("(p j) w -> p j w", j=PACK))
+
+        def load_w2(e):
+            nc.sync.dma_start(w2_raw[e][:], w2[e].rearrange("(p j) n -> p j n", j=PACK))
+
+        def load_gate(e):
+            nc.sync.dma_start(gate_sb[e][:], gate[:, e * C : (e + 1) * C])
+
+        for s in range(PASSES):
+            for h in range(2):
+                load_x(s, h)
+        for g in range(2):
+            for s in range(PASSES):
+                load_w(0, g, s, 0, H)
+        load_w2(0)
+        load_gate(0)
+        load_w(1, 0, 0, 0, H)
+        load_w(1, 0, 1, 0, H)
+        load_w(1, 1, 0, 0, H)
+        load_w(1, 1, 1, 0, H // 2)
+        load_w(1, 1, 1, H // 2, H)
+        load_w2(1)
+        load_gate(1)
+        nc.sync.dma_start(xr_sb[:], xr)
+
+        def cast(dst, src, cut):
+            if cut > 0:
+                nc.scalar.activation(dst[:, :cut], src[:, :cut], COPY)
+            if cut < dst.shape[1]:
+                nc.vector.tensor_copy(dst[:, cut:], src[:, cut:])
+
+        def cast_x(s, h, cut):
+            cast(
+                x_bf[s, h][:].rearrange("p (c i) t -> p c t i", i=4),
+                x_raw[s, h][:].rearrange("p t (c i) -> p c t i", i=4),
+                cut,
+            )
+
+        def cast_w(e, g, s, cut, lo=0, hi=H // 4):
+            dst = w_bf[e, g, s][:].rearrange("p (t m j) -> p m j t", t=4, j=4)
+            src = w_raw[e, g, s][:].rearrange("p j (m t) -> p m j t", t=4)
+            cast(dst[:, lo:hi], src[:, lo:hi], cut)
+
+        def cast_w2(e, cut):
+            cast(
+                w2_bf[e][:].rearrange("p (c i) t -> p c t i", i=4),
+                w2_raw[e][:].rearrange("p t (c i) -> p c t i", i=4),
+                cut,
+            )
+
+        def quant_x(s, h):
+            cols = slice(h * HALF, (h + 1) * HALF)
+            nc.vector.quantize_mx(
+                out=x_words[s][:, cols].bitcast(FP8X4),
+                scales=x_bytes[4 * s : P, cols],
+                in_=x_bf[s, h][:].rearrange("p w t -> p (w t)"),
+            )
+
+        def quant_w(e, g, s, lo=0, hi=H):
+            nc.vector.quantize_mx(
+                out=w_codes[e, g, s][:, lo:hi].bitcast(FP8X4),
+                scales=w_scales[e, g, s][:, lo:hi],
+                in_=w_bf[e, g, s][:, 4 * lo : 4 * hi],
+            )
+
+        def quant_w2(e):
+            nc.vector.quantize_mx(
+                out=w2_codes[e][:].bitcast(FP8X4),
+                scales=w2_scales[e][:],
+                in_=w2_bf[e][:].rearrange("p w t -> p (w t)"),
+            )
+
+        def product(e, g, b):
+            bank = psum.tile([P, 4, BLK], F32, name="bank")
+            cols = slice(e * C + b * BLK, e * C + (b + 1) * BLK)
+            for t in range(4):
+                for s in range(PASSES):
+                    nc.tensor.matmul_mx(
+                        out=bank[:, t, :],
+                        lhsT=w_codes[e, g, s][:, t * P : (t + 1) * P].bitcast(FP8X4),
+                        lhsT_scale=w_scales[e, g, s][:, t * P : (t + 1) * P],
+                        rhs=slot_words[s][:, cols].bitcast(FP8X4),
+                        rhs_scale=slot_bytes[4 * s : P, cols],
+                        start=(s == 0),
+                        stop=(s == PASSES - 1),
+                    )
+            return bank
+
+        relu_a = {}
+
+        def gate_half(e):
+            for b in range(2):
+                bank = product(e, 0, b)
+                relu_a[e, b] = keep.tile([P, 4, BLK], F32, name=f"relu{e}{b}")
+                nc.scalar.activation(relu_a[e, b][:], bank[:], RELU)
+
+        def up_half(e):
+            h_bf = [keep.tile([P, BLK, 4], BF16, name=f"h_bf{e}{b}", align_bytes=64) for b in range(2)]
+            h_codes = keep.tile([P, C], U32, name=f"h_codes{e}", align_bytes=64)
+            h_scales = keep.tile([P, C], U8, name=f"h_scales{e}", align_bytes=64)
+            for b in range(2):
+                bank = product(e, 1, b)
+                nc.vector.tensor_tensor(
+                    h_bf[b][:],
+                    bank[:].rearrange("p t n -> p n t"),
+                    relu_a[e, b][:].rearrange("p t n -> p n t"),
+                    MULT,
+                )
+            y_bank = psum_y.tile([P, C], F32, name="y_bank")
+            y_sb = keep.tile([P, C], F32, name=f"y_sb{e}")
+            for b in range(2):
+                cols = slice(b * BLK, (b + 1) * BLK)
+                nc.vector.quantize_mx(
+                    out=h_codes[:, cols].bitcast(FP8X4),
+                    scales=h_scales[:, cols],
+                    in_=h_bf[b][:].rearrange("p n t -> p (n t)"),
+                )
+                nc.tensor.matmul_mx(
+                    out=y_bank[:, cols],
+                    lhsT=w2_codes[e][:].bitcast(FP8X4),
+                    lhsT_scale=w2_scales[e][:],
+                    rhs=h_codes[:, cols].bitcast(FP8X4),
+                    rhs_scale=h_scales[:, cols],
+                    start=True,
+                    stop=True,
+                )
+            nc.scalar.activation(y_sb[:], y_bank[:], COPY)
+            return y_sb
+
+        def scatter(e, y_sb):
+            nc.vector.tensor_tensor(
+                window[:].indirect(offsets[:, e * C // 16 : (e + 1) * C // 16]),
+                y_sb[:],
+                gate_sb[e][:],
+                MULT,
+            )
+
+        cast_x(0, 0, 80)
+        cast_x(0, 1, 80)
+        quant_x(0, 0)
+        cast_x(1, 0, 80)
+        quant_x(0, 1)
+        cast_x(1, 1, 80)
+        quant_x(1, 0)
+        nc.vector.tensor_copy(slot_words[0][:], x_words[0][:].indirect(offsets[:]))
+        cast_w(0, 0, 0, 80)
+        quant_x(1, 1)
+        cast_w(0, 0, 1, 80)
+        quant_w(0, 0, 0)
+        nc.vector.tensor_copy(slot_words[1][:], x_words[1][:].indirect(offsets[:]))
+        nc.vector.tensor_copy(slot_bytes[:], x_bytes[:].indirect(offsets[:]))
+        cast_w(0, 1, 0, 80)
+        quant_w(0, 0, 1)
+        gate_half(0)
+        cast_w(0, 1, 1, 80)
+        quant_w(0, 1, 0)
+        cast_w2(0, 32)
+        cast_w(1, 0, 0, 80)
+        quant_w(0, 1, 1)
+        quant_w2(0)
+        y0 = up_half(0)
+        cast_w(1, 0, 1, 80)
+        quant_w(1, 0, 0)
+        scatter(0, y0)
+        cast_w(1, 1, 0, 80)
+        quant_w(1, 0, 1)
+        gate_half(1)
+        cast_w(1, 1, 1, 32, 0, 64)
+        quant_w(1, 1, 0)
+        cast_w(1, 1, 1, 24, 64, 128)
+        quant_w(1, 1, 1, 0, 256)
+        quant_w(1, 1, 1, 256, 512)
+        cast_w2(1, 32)
+        quant_w2(1)
+        y1 = up_half(1)
+        scatter(1, y1)
+        for q in range(2):
+            cols = slice(q * HALF, (q + 1) * HALF)
+            out_sb = keep.tile([P, HALF], F32, name=f"out_sb{q}")
+            nc.vector.tensor_tensor(out_sb[:], window[:, cols], xr_sb[:, cols], ADD)
+            nc.sync.dma_start(out[:, cols], out_sb[:])

@@ -67,9 +67,9 @@ def tile_moe_res_glu_relu_kernel(tc, xT, xr, w1, w3, w2, gate, offs, out):
 
         weights = (w1, w3)
 
-        def load_x(s, h):
-            rows = xT[s * K_PASS : (s + 1) * K_PASS, h * HALF : (h + 1) * HALF]
-            nc.sync.dma_start(x_raw[s, h][:], rows.rearrange("(p j) w -> p j w", j=PACK))
+        def load_x(s, h, lo=0, hi=HALF):
+            rows = xT[s * K_PASS : (s + 1) * K_PASS, h * HALF + lo : h * HALF + hi]
+            nc.sync.dma_start(x_raw[s, h][:, :, lo:hi], rows.rearrange("(p j) w -> p j w", j=PACK))
 
         def load_w(e, g, s, lo, hi):
             rows = weights[g][e][s * K_PASS : (s + 1) * K_PASS, lo:hi]
@@ -81,9 +81,11 @@ def tile_moe_res_glu_relu_kernel(tc, xT, xr, w1, w3, w2, gate, offs, out):
         def load_gate(e):
             nc.sync.dma_start(gate_sb[e][:], gate[:, e * C : (e + 1) * C])
 
-        for s in range(PASSES):
-            for h in range(2):
-                load_x(s, h)
+        load_x(0, 0, 0, 256)
+        load_x(0, 0, 256, 512)
+        load_x(0, 1)
+        load_x(1, 0)
+        load_x(1, 1)
         for g in range(2):
             for s in range(PASSES):
                 load_w(0, g, s, 0, H)
@@ -104,12 +106,10 @@ def tile_moe_res_glu_relu_kernel(tc, xT, xr, w1, w3, w2, gate, offs, out):
             if cut < dst.shape[1]:
                 nc.vector.tensor_copy(dst[:, cut:], src[:, cut:])
 
-        def cast_x(s, h, cut):
-            cast(
-                x_bf[s, h][:].rearrange("p (c i) t -> p c t i", i=4),
-                x_raw[s, h][:].rearrange("p t (c i) -> p c t i", i=4),
-                cut,
-            )
+        def cast_x(s, h, cut, lo=0, hi=HALF // 4):
+            dst = x_bf[s, h][:].rearrange("p (c i) t -> p c t i", i=4)
+            src = x_raw[s, h][:].rearrange("p t (c i) -> p c t i", i=4)
+            cast(dst[:, lo:hi], src[:, lo:hi], cut)
 
         def cast_w(e, g, s, cut, lo=0, hi=H // 4):
             dst = w_bf[e, g, s][:].rearrange("p (t m j) -> p m j t", t=4, j=4)
@@ -161,94 +161,117 @@ def tile_moe_res_glu_relu_kernel(tc, xT, xr, w1, w3, w2, gate, offs, out):
                     )
             return bank
 
-        relu_a = {}
+        banks, relu_a, h_bf, y_banks = {}, {}, {}, {}
+        h_codes = [keep.tile([P, C], U32, name=f"h_codes{e}", align_bytes=64) for e in range(E)]
+        h_scales = [keep.tile([P, C], U8, name=f"h_scales{e}", align_bytes=64) for e in range(E)]
+        y_sb = [keep.tile([P, C], F32, name=f"y_sb{e}") for e in range(E)]
 
-        def gate_half(e):
+        def products(e, g):
             for b in range(2):
-                bank = product(e, 0, b)
-                relu_a[e, b] = keep.tile([P, 4, BLK], F32, name=f"relu{e}{b}")
-                nc.scalar.activation(relu_a[e, b][:], bank[:], RELU)
+                banks[e, g, b] = product(e, g, b)
 
-        def up_half(e):
-            h_bf = [keep.tile([P, BLK, 4], BF16, name=f"h_bf{e}{b}", align_bytes=64) for b in range(2)]
-            h_codes = keep.tile([P, C], U32, name=f"h_codes{e}", align_bytes=64)
-            h_scales = keep.tile([P, C], U8, name=f"h_scales{e}", align_bytes=64)
-            for b in range(2):
-                bank = product(e, 1, b)
-                nc.vector.tensor_tensor(
-                    h_bf[b][:],
-                    bank[:].rearrange("p t n -> p n t"),
-                    relu_a[e, b][:].rearrange("p t n -> p n t"),
-                    MULT,
-                )
-            y_bank = psum_y.tile([P, C], F32, name="y_bank")
-            y_sb = keep.tile([P, C], F32, name=f"y_sb{e}")
-            for b in range(2):
-                cols = slice(b * BLK, (b + 1) * BLK)
-                nc.vector.quantize_mx(
-                    out=h_codes[:, cols].bitcast(FP8X4),
-                    scales=h_scales[:, cols],
-                    in_=h_bf[b][:].rearrange("p n t -> p (n t)"),
-                )
-                nc.tensor.matmul_mx(
-                    out=y_bank[:, cols],
-                    lhsT=w2_codes[e][:].bitcast(FP8X4),
-                    lhsT_scale=w2_scales[e][:],
-                    rhs=h_codes[:, cols].bitcast(FP8X4),
-                    rhs_scale=h_scales[:, cols],
-                    start=True,
-                    stop=True,
-                )
-            nc.scalar.activation(y_sb[:], y_bank[:], COPY)
-            return y_sb
+        def relu(e, b):
+            relu_a[e, b] = keep.tile([P, 4, BLK], F32, name=f"relu{e}{b}")
+            nc.scalar.activation(relu_a[e, b][:], banks[e, 0, b][:], RELU)
 
-        def scatter(e, y_sb):
+        def hmul(e, b):
+            h_bf[e, b] = keep.tile([P, BLK, 4], BF16, name=f"h_bf{e}{b}", align_bytes=64)
             nc.vector.tensor_tensor(
-                window[:].indirect(offsets[:, e * C // 16 : (e + 1) * C // 16]),
-                y_sb[:],
-                gate_sb[e][:],
+                h_bf[e, b][:],
+                banks[e, 1, b][:].rearrange("p t n -> p n t"),
+                relu_a[e, b][:].rearrange("p t n -> p n t"),
                 MULT,
             )
 
-        cast_x(0, 0, 80)
+        def down(e, b):
+            if b == 0:
+                y_banks[e] = psum_y.tile([P, C], F32, name="y_bank")
+            cols = slice(b * BLK, (b + 1) * BLK)
+            nc.vector.quantize_mx(
+                out=h_codes[e][:, cols].bitcast(FP8X4),
+                scales=h_scales[e][:, cols],
+                in_=h_bf[e, b][:].rearrange("p n t -> p (n t)"),
+            )
+            nc.tensor.matmul_mx(
+                out=y_banks[e][:, cols],
+                lhsT=w2_codes[e][:].bitcast(FP8X4),
+                lhsT_scale=w2_scales[e][:],
+                rhs=h_codes[e][:, cols].bitcast(FP8X4),
+                rhs_scale=h_scales[e][:, cols],
+                start=True,
+                stop=True,
+            )
+
+        def ycopy(e, lo=0, hi=C):
+            nc.scalar.activation(y_sb[e][:, lo:hi], y_banks[e][:, lo:hi], COPY)
+
+        def scatter(e, b):
+            first = e * C + b * BLK
+            cols = slice(b * BLK, (b + 1) * BLK)
+            nc.vector.tensor_tensor(
+                window[:].indirect(offsets[:, first // 16 : (first + BLK) // 16]),
+                y_sb[e][:, cols],
+                gate_sb[e][:, cols],
+                MULT,
+            )
+
+        cast_x(0, 0, 40, 0, 64)
+        cast_x(0, 0, 40, 64, 128)
         cast_x(0, 1, 80)
         quant_x(0, 0)
         cast_x(1, 0, 80)
         quant_x(0, 1)
-        cast_x(1, 1, 80)
-        quant_x(1, 0)
+        cast_x(1, 1, 90)
         nc.vector.tensor_copy(slot_words[0][:], x_words[0][:].indirect(offsets[:]))
-        cast_w(0, 0, 0, 80)
+        quant_x(1, 0)
+        cast_w(0, 0, 0, 90)
         quant_x(1, 1)
-        cast_w(0, 0, 1, 80)
-        quant_w(0, 0, 0)
         nc.vector.tensor_copy(slot_words[1][:], x_words[1][:].indirect(offsets[:]))
+        cast_w(0, 0, 1, 80)
         nc.vector.tensor_copy(slot_bytes[:], x_bytes[:].indirect(offsets[:]))
-        cast_w(0, 1, 0, 80)
+        quant_w(0, 0, 0)
+        cast_w(0, 1, 0, 70)
         quant_w(0, 0, 1)
-        gate_half(0)
-        cast_w(0, 1, 1, 80)
+        products(0, 0)
+        cast_w(0, 1, 1, 72)
         quant_w(0, 1, 0)
-        cast_w2(0, 32)
-        cast_w(1, 0, 0, 80)
+        relu(0, 0)
+        relu(0, 1)
+        cast_w2(0, 0)
         quant_w(0, 1, 1)
+        products(0, 1)
         quant_w2(0)
-        y0 = up_half(0)
-        cast_w(1, 0, 1, 80)
+        cast_w(1, 0, 0, 64)
+        hmul(0, 0)
+        hmul(0, 1)
         quant_w(1, 0, 0)
-        scatter(0, y0)
-        cast_w(1, 1, 0, 80)
+        cast_w(1, 0, 1, 64)
+        down(0, 0)
+        down(0, 1)
         quant_w(1, 0, 1)
-        gate_half(1)
-        cast_w(1, 1, 1, 32, 0, 64)
+        products(1, 0)
+        cast_w(1, 1, 0, 64)
+        ycopy(0)
+        cast_w(1, 1, 1, 28, 0, 64)
         quant_w(1, 1, 0)
-        cast_w(1, 1, 1, 24, 64, 128)
+        relu(1, 0)
+        relu(1, 1)
+        cast_w(1, 1, 1, 0, 64, 128)
         quant_w(1, 1, 1, 0, 256)
         quant_w(1, 1, 1, 256, 512)
+        products(1, 1)
         cast_w2(1, 32)
+        scatter(0, 0)
         quant_w2(1)
-        y1 = up_half(1)
-        scatter(1, y1)
+        hmul(1, 0)
+        hmul(1, 1)
+        down(1, 0)
+        down(1, 1)
+        scatter(0, 1)
+        ycopy(1, 0, 128)
+        ycopy(1, 128, 256)
+        scatter(1, 0)
+        scatter(1, 1)
         for q in range(2):
             cols = slice(q * HALF, (q + 1) * HALF)
             out_sb = keep.tile([P, HALF], F32, name=f"out_sb{q}")

@@ -33,14 +33,12 @@ def tile_moe_res_glu_relu_kernel(tc, xT, xr, w1, w3, w2, gate, offs, out):
         psum_y = ctx.enter_context(tc.psum_pool(name="psum_y", bufs=2))
 
         offsets = keep.tile([P, S // 16], U16, name="offsets")
-        nc.sync.dma_start(offsets[:], offs)
 
         x_raw = {}
         x_bf = {}
         for s in range(PASSES):
-            for h in range(2):
-                x_raw[s, h] = keep.tile([P, PACK, HALF], F32, name=f"x_raw{s}{h}")
-                x_bf[s, h] = keep.tile([P, HALF, PACK], BF16, name=f"x_bf{s}{h}", align_bytes=64)
+            x_raw[s] = keep.tile([P, PACK, T], F32, name=f"x_raw{s}")
+            x_bf[s] = keep.tile([P, T * PACK], BF16, name=f"x_bf{s}", align_bytes=64)
         x_words = [keep.tile([P, T], U32, name=f"x_words{s}", align_bytes=64) for s in range(PASSES)]
         x_bytes = keep.tile([P, T], U8, name="x_bytes", align_bytes=64)
         slot_words = [keep.tile([P, S], U32, name=f"slot_words{s}", align_bytes=64) for s in range(PASSES)]
@@ -62,42 +60,36 @@ def tile_moe_res_glu_relu_kernel(tc, xT, xr, w1, w3, w2, gate, offs, out):
         w2_bf = [keep.tile([P, N, PACK], BF16, name=f"w2_bf{e}", align_bytes=64) for e in range(E)]
         w2_codes = [keep.tile([P, N], U32, name=f"w2_codes{e}", align_bytes=64) for e in range(E)]
         w2_scales = [keep.tile([P, N], U8, name=f"w2_scales{e}", align_bytes=64) for e in range(E)]
-        gate_sb = [keep.tile([P, C], F32, name=f"gate{e}") for e in range(E)]
+        gate_sb = keep.tile([P, S], F32, name="gate_sb")
         xr_sb = keep.tile([P, T], F32, name="xr_sb")
 
         weights = (w1, w3)
 
-        def load_x(s, h, lo=0, hi=HALF):
-            rows = xT[s * K_PASS : (s + 1) * K_PASS, h * HALF + lo : h * HALF + hi]
-            nc.sync.dma_start(x_raw[s, h][:, :, lo:hi], rows.rearrange("(p j) w -> p j w", j=PACK))
+        def load_x(s):
+            rows = xT[s * K_PASS : (s + 1) * K_PASS, :]
+            nc.sync.dma_start(x_raw[s][:], rows.rearrange("(p j) w -> p j w", j=PACK))
 
-        def load_w(e, g, s, lo, hi):
-            rows = weights[g][e][s * K_PASS : (s + 1) * K_PASS, lo:hi]
-            nc.sync.dma_start(w_raw[e, g, s][:, :, lo:hi], rows.rearrange("(p j) w -> p j w", j=PACK))
+        def load_w(e, g, s):
+            rows = weights[g][e][s * K_PASS : (s + 1) * K_PASS, :]
+            nc.sync.dma_start(w_raw[e, g, s][:], rows.rearrange("(p j) w -> p j w", j=PACK))
 
         def load_w2(e):
             nc.sync.dma_start(w2_raw[e][:], w2[e].rearrange("(p j) n -> p j n", j=PACK))
 
-        def load_gate(e):
-            nc.sync.dma_start(gate_sb[e][:], gate[:, e * C : (e + 1) * C])
-
-        load_x(0, 0, 0, 256)
-        load_x(0, 0, 256, 512)
-        load_x(0, 1)
-        load_x(1, 0)
-        load_x(1, 1)
-        for g in range(2):
-            for s in range(PASSES):
-                load_w(0, g, s, 0, H)
+        load_w(0, 0, 0)
+        nc.sync.dma_start(offsets[:], offs)
+        load_x(0)
+        load_w(0, 0, 1)
+        load_x(1)
+        load_w(0, 1, 0)
+        load_w(0, 1, 1)
         load_w2(0)
-        load_gate(0)
-        load_w(1, 0, 0, 0, H)
-        load_w(1, 0, 1, 0, H)
-        load_w(1, 1, 0, 0, H)
-        load_w(1, 1, 1, 0, H // 2)
-        load_w(1, 1, 1, H // 2, H)
+        load_w(1, 0, 0)
+        load_w(1, 0, 1)
+        load_w(1, 1, 0)
+        load_w(1, 1, 1)
         load_w2(1)
-        load_gate(1)
+        nc.sync.dma_start(gate_sb[:], gate)
         nc.sync.dma_start(xr_sb[:], xr)
 
         def cast(dst, src, cut):
@@ -106,10 +98,11 @@ def tile_moe_res_glu_relu_kernel(tc, xT, xr, w1, w3, w2, gate, offs, out):
             if cut < dst.shape[1]:
                 nc.vector.tensor_copy(dst[:, cut:], src[:, cut:])
 
-        def cast_x(s, h, cut, lo=0, hi=HALF // 4):
-            dst = x_bf[s, h][:].rearrange("p (c i) t -> p c t i", i=4)
-            src = x_raw[s, h][:].rearrange("p t (c i) -> p c t i", i=4)
-            cast(dst[:, lo:hi], src[:, lo:hi], cut)
+        def cast_x(s, h, cut):
+            cols = slice(h * (HALF // 4), (h + 1) * (HALF // 4))
+            dst = x_bf[s][:].rearrange("p (c i t) -> p c t i", i=4, t=PACK)
+            src = x_raw[s][:].rearrange("p t (c i) -> p c t i", i=4)
+            cast(dst[:, cols], src[:, cols], cut)
 
         def cast_w(e, g, s, cut, lo=0, hi=H // 4):
             dst = w_bf[e, g, s][:].rearrange("p (t m j) -> p m j t", t=4, j=4)
@@ -128,7 +121,7 @@ def tile_moe_res_glu_relu_kernel(tc, xT, xr, w1, w3, w2, gate, offs, out):
             nc.vector.quantize_mx(
                 out=x_words[s][:, cols].bitcast(FP8X4),
                 scales=x_bytes[4 * s : P, cols],
-                in_=x_bf[s, h][:].rearrange("p w t -> p (w t)"),
+                in_=x_bf[s][:, h * HALF * PACK : (h + 1) * HALF * PACK],
             )
 
         def quant_w(e, g, s, lo=0, hi=H):
@@ -171,15 +164,16 @@ def tile_moe_res_glu_relu_kernel(tc, xT, xr, w1, w3, w2, gate, offs, out):
                 banks[e, g, b] = product(e, g, b)
 
         def relu(e, b):
-            relu_a[e, b] = keep.tile([P, 4, BLK], F32, name=f"relu{e}{b}")
-            nc.scalar.activation(relu_a[e, b][:], banks[e, 0, b][:], RELU)
+            relu_a[e, b] = keep.tile([P, BLK, 4], F32, name=f"relu{e}{b}")
+            nc.scalar.activation(relu_a[e, b][:], banks[e, 0, b][:].rearrange("p t n -> p n t"), RELU)
 
         def hmul(e, b):
-            h_bf[e, b] = keep.tile([P, BLK, 4], BF16, name=f"h_bf{e}{b}", align_bytes=64)
+            if b == 0:
+                h_bf[e] = keep.tile([P, C, 4], BF16, name=f"h_bf{e}", align_bytes=64)
             nc.vector.tensor_tensor(
-                h_bf[e, b][:],
+                h_bf[e][:, b * BLK : (b + 1) * BLK, :],
                 banks[e, 1, b][:].rearrange("p t n -> p n t"),
-                relu_a[e, b][:].rearrange("p t n -> p n t"),
+                relu_a[e, b][:],
                 MULT,
             )
 
@@ -190,7 +184,7 @@ def tile_moe_res_glu_relu_kernel(tc, xT, xr, w1, w3, w2, gate, offs, out):
             nc.vector.quantize_mx(
                 out=h_codes[e][:, cols].bitcast(FP8X4),
                 scales=h_scales[e][:, cols],
-                in_=h_bf[e, b][:].rearrange("p n t -> p (n t)"),
+                in_=h_bf[e][:, cols, :].rearrange("p n t -> p (n t)"),
             )
             nc.tensor.matmul_mx(
                 out=y_banks[e][:, cols],
@@ -198,6 +192,23 @@ def tile_moe_res_glu_relu_kernel(tc, xT, xr, w1, w3, w2, gate, offs, out):
                 lhsT_scale=w2_scales[e][:],
                 rhs=h_codes[e][:, cols].bitcast(FP8X4),
                 rhs_scale=h_scales[e][:, cols],
+                start=True,
+                stop=True,
+            )
+
+        def down_both(e):
+            y_banks[e] = psum_y.tile([P, C], F32, name="y_bank")
+            nc.vector.quantize_mx(
+                out=h_codes[e][:].bitcast(FP8X4),
+                scales=h_scales[e][:],
+                in_=h_bf[e][:].rearrange("p n t -> p (n t)"),
+            )
+            nc.tensor.matmul_mx(
+                out=y_banks[e][:],
+                lhsT=w2_codes[e][:].bitcast(FP8X4),
+                lhsT_scale=w2_scales[e][:],
+                rhs=h_codes[e][:].bitcast(FP8X4),
+                rhs_scale=h_scales[e][:],
                 start=True,
                 stop=True,
             )
@@ -211,63 +222,59 @@ def tile_moe_res_glu_relu_kernel(tc, xT, xr, w1, w3, w2, gate, offs, out):
             nc.vector.tensor_tensor(
                 window[:].indirect(offsets[:, first // 16 : (first + BLK) // 16]),
                 y_sb[e][:, cols],
-                gate_sb[e][:, cols],
+                gate_sb[:, first : first + BLK],
                 MULT,
             )
 
-        cast_x(0, 0, 40, 0, 64)
-        cast_x(0, 0, 40, 64, 128)
-        cast_x(0, 1, 80)
+        cast_w(0, 0, 0, 64)
+        cast_x(0, 0, 64)
+        cast_x(0, 1, 64)
+        quant_w(0, 0, 0)
+        cast_w(0, 0, 1, 80)
         quant_x(0, 0)
-        cast_x(1, 0, 80)
         quant_x(0, 1)
-        cast_x(1, 1, 90)
         nc.vector.tensor_copy(slot_words[0][:], x_words[0][:].indirect(offsets[:]))
+        cast_x(1, 0, 64)
+        cast_x(1, 1, 72)
+        quant_w(0, 0, 1)
         quant_x(1, 0)
-        cast_w(0, 0, 0, 90)
         quant_x(1, 1)
         nc.vector.tensor_copy(slot_words[1][:], x_words[1][:].indirect(offsets[:]))
-        cast_w(0, 0, 1, 80)
         nc.vector.tensor_copy(slot_bytes[:], x_bytes[:].indirect(offsets[:]))
-        quant_w(0, 0, 0)
-        cast_w(0, 1, 0, 70)
-        quant_w(0, 0, 1)
         products(0, 0)
-        cast_w(0, 1, 1, 72)
+        cast_w(0, 1, 0, 80)
+        cast_w(0, 1, 1, 80)
         quant_w(0, 1, 0)
         relu(0, 0)
         relu(0, 1)
-        cast_w2(0, 0)
         quant_w(0, 1, 1)
         products(0, 1)
+        cast_w2(0, 32)
         quant_w2(0)
-        cast_w(1, 0, 0, 64)
+        cast_w(1, 0, 0, 72)
         hmul(0, 0)
         hmul(0, 1)
         quant_w(1, 0, 0)
-        cast_w(1, 0, 1, 64)
-        down(0, 0)
-        down(0, 1)
+        cast_w(1, 0, 1, 72)
+        down_both(0)
+        ycopy(0)
         quant_w(1, 0, 1)
         products(1, 0)
-        cast_w(1, 1, 0, 64)
-        ycopy(0)
-        cast_w(1, 1, 1, 28, 0, 64)
+        scatter(0, 0)
+        cast_w(1, 1, 0, 72)
+        scatter(0, 1)
         quant_w(1, 1, 0)
         relu(1, 0)
         relu(1, 1)
-        cast_w(1, 1, 1, 0, 64, 128)
-        quant_w(1, 1, 1, 0, 256)
-        quant_w(1, 1, 1, 256, 512)
+        cast_w(1, 1, 1, 40)
+        quant_w(1, 1, 1)
         products(1, 1)
         cast_w2(1, 32)
-        scatter(0, 0)
         quant_w2(1)
         hmul(1, 0)
-        hmul(1, 1)
         down(1, 0)
+        hmul(1, 1)
         down(1, 1)
-        scatter(0, 1)
         ycopy(1, 0, 128)
         ycopy(1, 128, 256)
         scatter(1, 0)

@@ -76,11 +76,11 @@ def tile_moe_res_glu_relu_kernel(tc, xT, xr, w1, w3, w2, gate, offs, out):
         def load_w2(e):
             nc.sync.dma_start(w2_raw[e][:], w2[e].rearrange("(p j) n -> p j n", j=PACK))
 
-        load_w(0, 0, 0)
-        nc.sync.dma_start(offsets[:], offs)
         load_x(0)
-        load_w(0, 0, 1)
+        nc.sync.dma_start(offsets[:], offs)
         load_x(1)
+        load_w(0, 0, 0)
+        load_w(0, 0, 1)
         load_w(0, 1, 0)
         load_w(0, 1, 1)
         load_w2(0)
@@ -226,58 +226,58 @@ def tile_moe_res_glu_relu_kernel(tc, xT, xr, w1, w3, w2, gate, offs, out):
                 MULT,
             )
 
-        cast_w(0, 0, 0, 64)
-        cast_x(0, 0, 64)
-        cast_x(0, 1, 64)
-        quant_w(0, 0, 0)
-        cast_w(0, 0, 1, 80)
-        quant_x(0, 0)
+        cast_x(0, 1, 52)
         quant_x(0, 1)
+        cast_x(0, 0, 80)
+        quant_x(0, 0)
         nc.vector.tensor_copy(slot_words[0][:], x_words[0][:].indirect(offsets[:]))
-        cast_x(1, 0, 64)
-        cast_x(1, 1, 72)
-        quant_w(0, 0, 1)
-        quant_x(1, 0)
+        cast_x(1, 1, 120)
+        cast_x(1, 0, 4)
         quant_x(1, 1)
-        nc.vector.tensor_copy(slot_words[1][:], x_words[1][:].indirect(offsets[:]))
+        quant_x(1, 0)
+        cast_w(0, 0, 0, 100)
+        quant_w(0, 0, 0)
+        cast_w(0, 0, 1, 128)
         nc.vector.tensor_copy(slot_bytes[:], x_bytes[:].indirect(offsets[:]))
-        products(0, 0)
-        cast_w(0, 1, 0, 80)
-        cast_w(0, 1, 1, 80)
+        nc.vector.tensor_copy(slot_words[1][:], x_words[1][:].indirect(offsets[:]))
+        cast_w(0, 1, 0, 128)
+        quant_w(0, 0, 1)
+        cast_w(0, 1, 1, 48)
         quant_w(0, 1, 0)
+        quant_w(0, 1, 1)
+        products(0, 0)
         relu(0, 0)
         relu(0, 1)
-        quant_w(0, 1, 1)
         products(0, 1)
-        cast_w2(0, 32)
+        cast_w2(0, 0)
         quant_w2(0)
-        cast_w(1, 0, 0, 72)
+        cast_w(1, 0, 0, 92)
         hmul(0, 0)
         hmul(0, 1)
+        cast_w(1, 0, 1, 120)
         quant_w(1, 0, 0)
-        cast_w(1, 0, 1, 72)
         down_both(0)
-        ycopy(0)
-        quant_w(1, 0, 1)
-        products(1, 0)
-        scatter(0, 0)
-        cast_w(1, 1, 0, 72)
-        scatter(0, 1)
+        cast_w(1, 1, 0, 44)
         quant_w(1, 1, 0)
-        relu(1, 0)
-        relu(1, 1)
-        cast_w(1, 1, 1, 40)
+        quant_w(1, 0, 1)
+        cast_w(1, 1, 1, 44)
+        products(1, 0)
         quant_w(1, 1, 1)
+        ycopy(0)
         products(1, 1)
-        cast_w2(1, 32)
-        quant_w2(1)
+        relu(1, 0)
+        cast_w2(1, 0)
+        relu(1, 1)
+        scatter(0, 1)
         hmul(1, 0)
+        scatter(0, 0)
+        quant_w2(1)
         down(1, 0)
         hmul(1, 1)
-        down(1, 1)
         ycopy(1, 0, 128)
-        ycopy(1, 128, 256)
         scatter(1, 0)
+        down(1, 1)
+        ycopy(1, 128, 256)
         scatter(1, 1)
         for q in range(2):
             cols = slice(q * HALF, (q + 1) * HALF)

@@ -216,30 +216,29 @@ def tile_moe_res_glu_relu_kernel(tc, xT, xr, w1, w3, w2, gate, offs, out):
         def ycopy(e, lo=0, hi=C):
             nc.scalar.activation(y_sb[e][:, lo:hi], y_banks[e][:, lo:hi], COPY)
 
-        def scatter(e, b):
-            first = e * C + b * BLK
-            cols = slice(b * BLK, (b + 1) * BLK)
+        def scatter(e, lo, hi):
+            first, last = e * C + lo, e * C + hi
             nc.vector.tensor_tensor(
-                window[:].indirect(offsets[:, first // 16 : (first + BLK) // 16]),
-                y_sb[e][:, cols],
-                gate_sb[:, first : first + BLK],
+                window[:].indirect(offsets[:, first // 16 : last // 16]),
+                y_sb[e][:, lo:hi],
+                gate_sb[:, first:last],
                 MULT,
             )
 
-        cast_x(0, 1, 52)
+        cast_x(0, 1, 44)
         quant_x(0, 1)
-        cast_x(0, 0, 80)
+        cast_x(0, 0, 64)
         quant_x(0, 0)
         nc.vector.tensor_copy(slot_words[0][:], x_words[0][:].indirect(offsets[:]))
-        cast_x(1, 1, 120)
+        cast_x(1, 1, 128)
         cast_x(1, 0, 4)
-        quant_x(1, 1)
         quant_x(1, 0)
         cast_w(0, 0, 0, 100)
-        quant_w(0, 0, 0)
-        cast_w(0, 0, 1, 128)
-        nc.vector.tensor_copy(slot_bytes[:], x_bytes[:].indirect(offsets[:]))
+        quant_x(1, 1)
+        cast_w(0, 0, 1, 116)
         nc.vector.tensor_copy(slot_words[1][:], x_words[1][:].indirect(offsets[:]))
+        nc.vector.tensor_copy(slot_bytes[:], x_bytes[:].indirect(offsets[:]))
+        quant_w(0, 0, 0)
         cast_w(0, 1, 0, 128)
         quant_w(0, 0, 1)
         cast_w(0, 1, 1, 48)
@@ -247,38 +246,37 @@ def tile_moe_res_glu_relu_kernel(tc, xT, xr, w1, w3, w2, gate, offs, out):
         quant_w(0, 1, 1)
         products(0, 0)
         relu(0, 0)
-        relu(0, 1)
         products(0, 1)
         cast_w2(0, 0)
         quant_w2(0)
-        cast_w(1, 0, 0, 92)
+        relu(0, 1)
+        cast_w(1, 0, 0, 84)
+        quant_w(1, 0, 0)
         hmul(0, 0)
         hmul(0, 1)
-        cast_w(1, 0, 1, 120)
-        quant_w(1, 0, 0)
+        cast_w(1, 0, 1, 88)
         down_both(0)
-        cast_w(1, 1, 0, 44)
+        cast_w(1, 1, 0, 28)
         quant_w(1, 1, 0)
         quant_w(1, 0, 1)
-        cast_w(1, 1, 1, 44)
+        cast_w(1, 1, 1, 36)
         products(1, 0)
         quant_w(1, 1, 1)
-        ycopy(0)
         products(1, 1)
+        ycopy(0)
         relu(1, 0)
         cast_w2(1, 0)
         relu(1, 1)
-        scatter(0, 1)
+        scatter(0, 0, C)
         hmul(1, 0)
-        scatter(0, 0)
         quant_w2(1)
         down(1, 0)
         hmul(1, 1)
         ycopy(1, 0, 128)
-        scatter(1, 0)
+        scatter(1, 0, BLK)
         down(1, 1)
         ycopy(1, 128, 256)
-        scatter(1, 1)
+        scatter(1, BLK, C)
         for q in range(2):
             cols = slice(q * HALF, (q + 1) * HALF)
             out_sb = keep.tile([P, HALF], F32, name=f"out_sb{q}")

from contextlib import ExitStack

import concourse.mybir as mybir

K, T, E, C, H, N = 1024, 1024, 2, 256, 512, 128
S = E * C
FLOPS = 2 * S * (2 * K * H + H * N)

P = 128
PACK = 4
K_PASS = P * PACK
PASSES = K // K_PASS
BLK = 128
HALF = T // 2

F32 = mybir.dt.float32
BF16 = mybir.dt.bfloat16
U32 = mybir.dt.uint32
U16 = mybir.dt.uint16
U8 = mybir.dt.uint8
FP8X4 = mybir.dt.float8_e4m3fn_x4
COPY = mybir.ActivationFunctionType.Copy
RELU = mybir.ActivationFunctionType.Relu
MULT = mybir.AluOpType.mult
ADD = mybir.AluOpType.add


def tile_moe_res_glu_relu_kernel(tc, xT, xr, w1, w3, w2, gate, offs, out):
    nc = tc.nc
    with ExitStack() as ctx:
        keep = ctx.enter_context(tc.tile_pool(name="keep", bufs=1))
        psum = ctx.enter_context(tc.psum_pool(name="psum", bufs=6))
        psum_y = ctx.enter_context(tc.psum_pool(name="psum_y", bufs=2))

        offsets = keep.tile([P, S // 16], U16, name="offsets")

        x_raw = {}
        x_bf = {}
        for s in range(PASSES):
            x_raw[s] = keep.tile([P, PACK, T], F32, name=f"x_raw{s}")
            x_bf[s] = keep.tile([P, T * PACK], BF16, name=f"x_bf{s}", align_bytes=64)
        x_words = [keep.tile([P, T], U32, name=f"x_words{s}", align_bytes=64) for s in range(PASSES)]
        x_bytes = keep.tile([P, T], U8, name="x_bytes", align_bytes=64)
        slot_words = [keep.tile([P, S], U32, name=f"slot_words{s}", align_bytes=64) for s in range(PASSES)]
        slot_bytes = keep.tile([P, S], U8, name="slot_bytes", align_bytes=64)
        window = keep.tile([P, T], F32, name="window")
        nc.gpsimd.memset(x_bytes[:], 0)
        nc.gpsimd.memset(window[:], 0.0)

        w_raw, w_bf, w_codes, w_scales = {}, {}, {}, {}
        for e in range(E):
            for g in range(2):
                for s in range(PASSES):
                    key = (e, g, s)
                    w_raw[key] = keep.tile([P, PACK, H], F32, name=f"w_raw{e}{g}{s}")
                    w_bf[key] = keep.tile([P, H * PACK], BF16, name=f"w_bf{e}{g}{s}", align_bytes=64)
                    w_codes[key] = keep.tile([P, H], U32, name=f"w_codes{e}{g}{s}", align_bytes=64)
                    w_scales[key] = keep.tile([P, H], U8, name=f"w_scales{e}{g}{s}", align_bytes=64)
        w2_raw = [keep.tile([P, PACK, N], F32, name=f"w2_raw{e}") for e in range(E)]
        w2_bf = [keep.tile([P, N, PACK], BF16, name=f"w2_bf{e}", align_bytes=64) for e in range(E)]
        w2_codes = [keep.tile([P, N], U32, name=f"w2_codes{e}", align_bytes=64) for e in range(E)]
        w2_scales = [keep.tile([P, N], U8, name=f"w2_scales{e}", align_bytes=64) for e in range(E)]
        gate_sb = keep.tile([P, S], F32, name="gate_sb")
        xr_sb = keep.tile([P, T], F32, name="xr_sb")

        weights = (w1, w3)

        def load_x(s):
            rows = xT[s * K_PASS : (s + 1) * K_PASS, :]
            nc.sync.dma_start(x_raw[s][:], rows.rearrange("(p j) w -> p j w", j=PACK))

        def load_w(e, g, s):
            rows = weights[g][e][s * K_PASS : (s + 1) * K_PASS, :]
            nc.sync.dma_start(w_raw[e, g, s][:], rows.rearrange("(p j) w -> p j w", j=PACK))

        def load_w2(e):
            nc.sync.dma_start(w2_raw[e][:], w2[e].rearrange("(p j) n -> p j n", j=PACK))

        load_x(0)
        nc.sync.dma_start(offsets[:], offs)
        load_x(1)
        load_w(0, 0, 0)
        load_w(0, 0, 1)
        load_w(0, 1, 0)
        load_w(0, 1, 1)
        load_w2(0)
        load_w(1, 0, 0)
        load_w(1, 0, 1)
        load_w(1, 1, 0)
        load_w(1, 1, 1)
        load_w2(1)
        nc.sync.dma_start(gate_sb[:], gate)
        nc.sync.dma_start(xr_sb[:], xr)

        def cast(dst, src, cut):
            if cut > 0:
                nc.scalar.activation(dst[:, :cut], src[:, :cut], COPY)
            if cut < dst.shape[1]:
                nc.vector.tensor_copy(dst[:, cut:], src[:, cut:])

        def cast_x(s, h, cut):
            cols = slice(h * (HALF // 4), (h + 1) * (HALF // 4))
            dst = x_bf[s][:].rearrange("p (c i t) -> p c t i", i=4, t=PACK)
            src = x_raw[s][:].rearrange("p t (c i) -> p c t i", i=4)
            cast(dst[:, cols], src[:, cols], cut)

        def cast_w(e, g, s, cut, lo=0, hi=H // 4):
            dst = w_bf[e, g, s][:].rearrange("p (t m j) -> p m j t", t=4, j=4)
            src = w_raw[e, g, s][:].rearrange("p j (m t) -> p m j t", t=4)
            cast(dst[:, lo:hi], src[:, lo:hi], cut)

        def cast_w2(e, cut):
            cast(
                w2_bf[e][:].rearrange("p (c i) t -> p c t i", i=4),
                w2_raw[e][:].rearrange("p t (c i) -> p c t i", i=4),
                cut,
            )

        def quant_x(s, h):
            cols = slice(h * HALF, (h + 1) * HALF)
            nc.vector.quantize_mx(
                out=x_words[s][:, cols].bitcast(FP8X4),
                scales=x_bytes[4 * s : P, cols],
                in_=x_bf[s][:, h * HALF * PACK : (h + 1) * HALF * PACK],
            )

        def quant_w(e, g, s, lo=0, hi=H):
            nc.vector.quantize_mx(
                out=w_codes[e, g, s][:, lo:hi].bitcast(FP8X4),
                scales=w_scales[e, g, s][:, lo:hi],
                in_=w_bf[e, g, s][:, 4 * lo : 4 * hi],
            )

        def quant_w2(e):
            nc.vector.quantize_mx(
                out=w2_codes[e][:].bitcast(FP8X4),
                scales=w2_scales[e][:],
                in_=w2_bf[e][:].rearrange("p w t -> p (w t)"),
            )

        def product(e, g, b):
            bank = psum.tile([P, 4, BLK], F32, name="bank")
            cols = slice(e * C + b * BLK, e * C + (b + 1) * BLK)
            for t in range(4):
                for s in range(PASSES):
                    nc.tensor.matmul_mx(
                        out=bank[:, t, :],
                        lhsT=w_codes[e, g, s][:, t * P : (t + 1) * P].bitcast(FP8X4),
                        lhsT_scale=w_scales[e, g, s][:, t * P : (t + 1) * P],
                        rhs=slot_words[s][:, cols].bitcast(FP8X4),
                        rhs_scale=slot_bytes[4 * s : P, cols],
                        start=(s == 0),
                        stop=(s == PASSES - 1),
                    )
            return bank

        banks, relu_a, h_bf, y_banks = {}, {}, {}, {}
        h_codes = [keep.tile([P, C], U32, name=f"h_codes{e}", align_bytes=64) for e in range(E)]
        h_scales = [keep.tile([P, C], U8, name=f"h_scales{e}", align_bytes=64) for e in range(E)]
        y_sb = [keep.tile([P, C], F32, name=f"y_sb{e}") for e in range(E)]

        def products(e, g):
            for b in range(2):
                banks[e, g, b] = product(e, g, b)

        def relu(e, b):
            relu_a[e, b] = keep.tile([P, BLK, 4], F32, name=f"relu{e}{b}")
            nc.scalar.activation(relu_a[e, b][:], banks[e, 0, b][:].rearrange("p t n -> p n t"), RELU)

        def hmul(e, b):
            if b == 0:
                h_bf[e] = keep.tile([P, C, 4], BF16, name=f"h_bf{e}", align_bytes=64)
            nc.vector.tensor_tensor(
                h_bf[e][:, b * BLK : (b + 1) * BLK, :],
                banks[e, 1, b][:].rearrange("p t n -> p n t"),
                relu_a[e, b][:],
                MULT,
            )

        def down(e, b):
            if b == 0:
                y_banks[e] = psum_y.tile([P, C], F32, name="y_bank")
            cols = slice(b * BLK, (b + 1) * BLK)
            nc.vector.quantize_mx(
                out=h_codes[e][:, cols].bitcast(FP8X4),
                scales=h_scales[e][:, cols],
                in_=h_bf[e][:, cols, :].rearrange("p n t -> p (n t)"),
            )
            nc.tensor.matmul_mx(
                out=y_banks[e][:, cols],
                lhsT=w2_codes[e][:].bitcast(FP8X4),
                lhsT_scale=w2_scales[e][:],
                rhs=h_codes[e][:, cols].bitcast(FP8X4),
                rhs_scale=h_scales[e][:, cols],
                start=True,
                stop=True,
            )

        def down_both(e):
            y_banks[e] = psum_y.tile([P, C], F32, name="y_bank")
            nc.vector.quantize_mx(
                out=h_codes[e][:].bitcast(FP8X4),
                scales=h_scales[e][:],
                in_=h_bf[e][:].rearrange("p n t -> p (n t)"),
            )
            nc.tensor.matmul_mx(
                out=y_banks[e][:],
                lhsT=w2_codes[e][:].bitcast(FP8X4),
                lhsT_scale=w2_scales[e][:],
                rhs=h_codes[e][:].bitcast(FP8X4),
                rhs_scale=h_scales[e][:],
                start=True,
                stop=True,
            )

        def ycopy(e, lo=0, hi=C):
            nc.scalar.activation(y_sb[e][:, lo:hi], y_banks[e][:, lo:hi], COPY)

        def scatter(e, lo, hi):
            first, last = e * C + lo, e * C + hi
            nc.vector.tensor_tensor(
                window[:].indirect(offsets[:, first // 16 : last // 16]),
                y_sb[e][:, lo:hi],
                gate_sb[:, first:last],
                MULT,
            )

        cast_x(0, 1, 44)
        quant_x(0, 1)
        cast_x(0, 0, 64)
        quant_x(0, 0)
        nc.vector.tensor_copy(slot_words[0][:], x_words[0][:].indirect(offsets[:]))
        cast_x(1, 1, 128)
        cast_x(1, 0, 4)
        quant_x(1, 0)
        cast_w(0, 0, 0, 100)
        quant_x(1, 1)
        cast_w(0, 0, 1, 116)
        nc.vector.tensor_copy(slot_words[1][:], x_words[1][:].indirect(offsets[:]))
        nc.vector.tensor_copy(slot_bytes[:], x_bytes[:].indirect(offsets[:]))
        quant_w(0, 0, 0)
        cast_w(0, 1, 0, 128)
        quant_w(0, 0, 1)
        cast_w(0, 1, 1, 48)
        quant_w(0, 1, 0)
        quant_w(0, 1, 1)
        products(0, 0)
        relu(0, 0)
        products(0, 1)
        cast_w2(0, 0)
        quant_w2(0)
        relu(0, 1)
        cast_w(1, 0, 0, 84)
        quant_w(1, 0, 0)
        hmul(0, 0)
        hmul(0, 1)
        cast_w(1, 0, 1, 88)
        down_both(0)
        cast_w(1, 1, 0, 28)
        quant_w(1, 1, 0)
        quant_w(1, 0, 1)
        cast_w(1, 1, 1, 36)
        products(1, 0)
        quant_w(1, 1, 1)
        products(1, 1)
        ycopy(0)
        relu(1, 0)
        cast_w2(1, 0)
        relu(1, 1)
        scatter(0, 0, C)
        hmul(1, 0)
        quant_w2(1)
        down(1, 0)
        hmul(1, 1)
        ycopy(1, 0, 128)
        scatter(1, 0, BLK)
        down(1, 1)
        ycopy(1, 128, 256)
        scatter(1, BLK, C)
        for q in range(2):
            cols = slice(q * HALF, (q + 1) * HALF)
            out_sb = keep.tile([P, HALF], F32, name=f"out_sb{q}")
            nc.vector.tensor_tensor(out_sb[:], window[:, cols], xr_sb[:, cols], ADD)
            nc.sync.dma_start(out[:, cols], out_sb[:])
